import numpy as np
import ml_dtypes


def mxq(x, axis, fmt="e4m3"):
    dtype, down = {"e4m3": (ml_dtypes.float8_e4m3fn, 7), "e5m2": (ml_dtypes.float8_e5m2, 14)}[fmt]
    v = np.moveaxis(np.asarray(x, np.float32).astype(ml_dtypes.bfloat16).astype(np.float64), axis, -1)
    blocks = v.reshape(v.shape[:-1] + (-1, 32))
    amax = np.abs(blocks).max(-1, keepdims=True)
    byte = np.maximum(np.where(amax > 0, np.frexp(amax)[1] - 1 + 127, 0) - down, 1)
    scale = np.exp2(byte - 127.0)
    codes = (blocks / scale).astype(np.float32).astype(dtype).astype(np.float64)
    return np.moveaxis((codes * scale).reshape(v.shape), -1, axis)


WIDE = False


def mx_kscale(k):
    if not WIDE:
        return np.ones(k)
    levels = np.array([10, -10, 5, -5, 0])
    if k % 512:
        return np.exp2(np.random.permutation(np.resize(levels, k // 32))).repeat(32)
    a = np.empty((k // 512, 16))
    for p in range(k // 512):
        a[p, :8] = np.random.permutation(np.resize(levels, 8))
        for g in range(8):
            far = levels[np.abs(levels - a[p, g]) >= 10]
            a[p, g + 8] = far[np.random.randint(len(far))]
    return np.exp2(a.ravel()).repeat(32)


def f64(x):
    return np.asarray(x).astype(np.float64)


def striped(idx):
    return np.tile(idx.reshape(-1, 16).T, (8, 1)).astype(np.uint16)


def unstriped(offs):
    return offs[:16].T.reshape(-1).astype(np.int64)


E2M1 = np.array([0.0, 0.5, 1.0, 1.5, 2.0, 3.0, 4.0, 6.0, -0.0, -0.5, -1.0, -1.5, -2.0, -3.0, -4.0, -6.0])


def pack_weight(w, fmt):
    k, n = w.shape
    w = f64(np.asarray(w, np.float32).astype(ml_dtypes.bfloat16)).reshape(k // 32, 32, n)
    amax = np.abs(w).max(1)
    if fmt == "e4m3":
        byte = np.frexp(amax)[1] - 1 + 127 - 7
    else:
        mant, ex = np.frexp(amax / 6.0)
        byte = np.where(mant > 0.5, ex, ex - 1) + 127
    byte = np.clip(np.where(amax > 0, byte, 1), 1, 254)
    scaled = (w * np.exp2(127.0 - byte)[:, None, :]).reshape(k, n).astype(np.float32)
    by_word = np.ascontiguousarray(scaled.reshape(k // 512, 128, 4, n).transpose(0, 1, 3, 2))
    if fmt == "e4m3":
        words = by_word.astype(ml_dtypes.float8_e4m3fn).view(np.uint8)
    else:
        c = by_word.astype(ml_dtypes.float4_e2m1fn).view(np.uint8) & 0xF
        words = (c[..., 0::2] | (c[..., 1::2] << 4)).reshape(k // 512, 128, 2 * n)
    return np.ascontiguousarray(words), np.ascontiguousarray(byte.astype(np.uint8).reshape(k // 512, 16, n))


def unpack_weight(words, scales, fmt):
    g, _, n = scales.shape
    words = np.ascontiguousarray(words).reshape(g, 128, n, -1)
    if fmt == "e4m3":
        vals = words.view(ml_dtypes.float8_e4m3fn).astype(np.float64)
    else:
        nib = np.empty((g, 128, n, 4), np.uint8)
        nib[..., 0::2] = words & 0xF
        nib[..., 1::2] = words >> 4
        vals = E2M1[nib]
    vals = vals * np.repeat(np.exp2(scales.astype(np.float64) - 127.0), 8, axis=1)[..., None]
    return vals.transpose(0, 1, 3, 2).reshape(g * 512, n)


def gelu(v):
    return 0.5 * v * (1.0 + np.tanh(np.sqrt(2.0 / np.pi) * (v + 0.044715 * v**3)))


K, T, S, H, T2, P, N = 1024, 2048, 512, 1024, 1024, 512, 512

def setup_inputs():
    n = np.random.standard_normal
    s = mx_kscale(K)[:, None]
    u = mx_kscale(H)[:, None]
    tab_words, tab_scales = pack_weight(n((K, T)) * s, "e4m3")
    w4_words, w4_scales = pack_weight(n((K, H)) / np.sqrt(K) / s, "e2m1")
    gain = 1.3 * np.sign(n(H)) * np.exp(0.3 * n(H)) * u[:, 0]
    return {
        "tab_words": tab_words, "tab_scales": tab_scales,
        "w1": (0.55 * n((K, H)) / np.sqrt(K) / s).astype(np.float32),
        "w4_words": w4_words, "w4_scales": w4_scales,
        "gain": gain.astype(np.float32),
        "page0": (n((H, T2)) * u).astype(np.float32),
        "wgs": np.exp(0.3 * n((128, S))).astype(np.float32),
        "w2": (n((H, N)) / np.sqrt(H) / u).astype(np.float32),
        "bias": (0.5 * n(N)).astype(np.float32),
        "offs": striped(np.random.permutation(T)[:S]),
        "offs2": striped(np.random.permutation(T2)[:S]),
        "offs3": striped(np.random.permutation(T2)[:P]),
        "offs4": striped(np.random.permutation(T2)[:P]),
    }

def reference(tab_words, tab_scales, w1, w4_words, w4_scales, gain, page0, wgs, w2, bias, offs, offs2, offs3, offs4):
    v = unpack_weight(tab_words, tab_scales, "e4m3")[:, unstriped(offs)]
    w1q = mxq(f64(w1), 0, "e4m3")
    w4 = unpack_weight(w4_words, w4_scales, "e2m1")
    tone = np.cos(w1q.T @ v)
    b = w4.T @ v
    h = f64(gain)[:, None] * (tone * b + tone)
    before = f64(page0)
    page = before.copy()
    page[:, unstriped(offs2)] = np.tile(f64(wgs), (H // 128, 1)) * h
    x = np.minimum(page[:, unstriped(offs3)], before[:, unstriped(offs4)])
    xq = mxq(x, 0, "e4m3")
    w2q = mxq(f64(w2), 0, "e4m3")
    return (w2q.T @ xq) + f64(bias)[:, None]

@@ -1,0 +1,237 @@
+import math
+from contextlib import ExitStack
+
+import concourse.mybir as mybir
+
+K, T, S, H, T2, PICKS, N = 1024, 2048, 512, 1024, 1024, 512, 512
+FLOPS = 2 * (2 * K * H * S + H * N * PICKS)
+
+F32 = mybir.dt.float32
+BF16 = mybir.dt.bfloat16
+I32 = mybir.dt.int32
+U32 = mybir.dt.uint32
+U16 = mybir.dt.uint16
+U8 = mybir.dt.uint8
+FP8X4 = mybir.dt.float8_e4m3fn_x4
+FP4X4 = mybir.dt.float4_e2m1fn_x4
+ALU = mybir.AluOpType
+ACT = mybir.ActivationFunctionType
+
+P = 128
+PACK = 4
+PASS = P * PACK
+K_PASSES = K // PASS
+R_PASSES = H // PASS
+HALF = PICKS // 2
+
+
+def tile_list_lining_tapping_scores_kernel(
+    tc, tab_words, tab_scales, w1, w4_words, w4_scales, gain, page0, wgs, w2, bias, offs, offs2, offs3, offs4, out
+):
+    nc = tc.nc
+    with ExitStack() as ctx:
+        keep = ctx.enter_context(tc.tile_pool(name="keep", bufs=1))
+        ring = ctx.enter_context(tc.tile_pool(name="ring", bufs=2))
+        psum = ctx.enter_context(tc.psum_pool(name="psum", bufs=1))
+
+        def load_list(source, name):
+            tile = keep.tile([P, S // 16], U16, name=name)
+            nc.sync.dma_start(tile[:], source)
+            return tile
+
+        def load_weight(rows, name):
+            raw = ring.tile([P, PACK, PASS], F32, name=name, tag="raw", bufs=4)
+            nc.sync.dma_start(raw[:], rows.rearrange("(p j) c -> p j c", j=PACK))
+            return raw
+
+        def quantize_weight(raw, name):
+            dealt = ring.tile([P, PACK, P, PACK], BF16, name="dealt", align_bytes=64)
+            nc.scalar.copy(
+                dealt[:].rearrange("p t m j -> p m j t"), raw[:].rearrange("p j (m t) -> p m j t", t=PACK)
+            )
+            codes = keep.tile([P, PASS], U32, name=name + "_codes", align_bytes=64)
+            scales = keep.tile([P, PASS], U8, name=name + "_scales", align_bytes=64)
+            nc.vector.quantize_mx(codes[:].bitcast(FP8X4), scales[:], dealt[:].rearrange("p t m j -> p (t m j)"))
+            return codes, scales
+
+        def load_scale_rows(source, width, name):
+            plane = keep.tile([P, K_PASSES, width], U8, name=name, align_bytes=64)
+            nc.vector.memset(plane[:].bitcast(I32), 0)
+            rows = source.rearrange("a q c -> q a c").bitcast(I32)
+            for quad in range(4):
+                nc.scalar.dma_start(plane[32 * quad : 32 * quad + 4].bitcast(I32), rows[4 * quad : 4 * quad + 4])
+            return plane
+
+        def load_table(a):
+            words = keep.tile([P, T], U32, name=f"table{a}")
+            nc.sync.dma_start(words[:].bitcast(I32), tab_words[a].rearrange("p t i -> p (t i)").bitcast(I32))
+            return words
+
+        def load_page(b, t):
+            page = keep.tile([P, T2], F32, name=f"page{b}{t}")
+            nc.sync.dma_start(page[:], page0.rearrange("(b p t) c -> b t p c", p=P, t=PACK)[b, t])
+            return page
+
+        slices = [(b, t) for b in range(R_PASSES) for t in range(PACK)]
+
+        table_plane = load_scale_rows(tab_scales, T, "table_plane")
+        w4_plane = load_scale_rows(w4_scales, H, "w4_plane")
+        gain_sb = keep.tile([P, R_PASSES, PACK], F32, name="gain_sb")
+        nc.scalar.dma_start(gain_sb[:], gain.rearrange("(b p t) -> p b t", p=P, t=PACK))
+        bias_sb = keep.tile([P, PACK], F32, name="bias_sb")
+        nc.scalar.dma_start(bias_sb[:], bias.rearrange("(p t) -> p t", t=PACK))
+
+        picked = load_list(offs, "picked")
+        w1_raw = {}
+        table = {}
+        table[0] = load_table(0)
+        w1_raw[0, 0] = load_weight(w1[0:PASS, 0:PASS], "w1_raw00")
+        w4_raw = keep.tile([P, K_PASSES, 2 * H], U8, name="w4_raw")
+        nc.sync.dma_start(w4_raw[:].bitcast(I32), w4_words.rearrange("a p c -> p a c").bitcast(I32))
+        w1_raw[1, 0] = load_weight(w1[PASS : 2 * PASS, 0:PASS], "w1_raw10")
+        table[1] = load_table(1)
+        before_list = load_list(offs4, "before_list")
+        pages = {}
+        pages[0, 0] = load_page(0, 0)
+        put_list = load_list(offs2, "put_list")
+        after_list = load_list(offs3, "after_list")
+        pages[0, 1] = load_page(0, 1)
+        wgs_sb = keep.tile([P, PACK, S], F32, name="wgs_sb")
+        for quad in range(4):
+            nc.sync.dma_start(wgs_sb[32 * quad : 32 * quad + 32], wgs.rearrange("(u t) j -> u t j", t=PACK))
+        pages[0, 2] = load_page(0, 2)
+        pages[0, 3] = load_page(0, 3)
+        for a in range(K_PASSES):
+            w1_raw[a, 1] = load_weight(w1[a * PASS : (a + 1) * PASS, PASS : 2 * PASS], f"w1_raw{a}1")
+        for t in range(PACK):
+            pages[1, t] = load_page(1, t)
+        w2_raw = [load_weight(w2[b * PASS : (b + 1) * PASS, :], f"w2_raw{b}") for b in range(R_PASSES)]
+
+        minus_gain = keep.tile([P, R_PASSES, PACK], F32, name="minus_gain")
+        nc.scalar.mul(minus_gain[:], gain_sb[:], -1.0)
+
+        w1_mx = {}
+        v_words, v_scales = [], []
+        for a in range(K_PASSES):
+            w1_mx[a, 0] = quantize_weight(w1_raw[a, 0], f"w1_{a}0")
+            words = keep.tile([P, S], U32, name=f"v_words{a}", align_bytes=64)
+            nc.vector.tensor_copy(words[:], table[a][:].indirect(picked[:]))
+            scales = keep.tile([P, S], U8, name=f"v_scales{a}", align_bytes=64)
+            nc.vector.tensor_copy(scales[:], table_plane[:, a, :].indirect(picked[:]))
+            v_words.append(words)
+            v_scales.append(scales)
+
+        w4_codes = keep.tile([P, K_PASSES * R_PASSES, 2 * PASS], U8, name="w4_codes", align_bytes=64)
+        nc.vector.tensor_copy(
+            w4_codes[:].bitcast(U16).rearrange("p g (t m) -> p g m t", t=PACK),
+            w4_raw[:].bitcast(U16).rearrange("p a (b m t) -> p (a b) m t", b=R_PASSES, t=PACK),
+        )
+        w4_sc = keep.tile([P, K_PASSES * R_PASSES, PASS], U8, name="w4_sc", align_bytes=64)
+        nc.vector.tensor_copy(
+            w4_sc[:].rearrange("p g (t m) -> p g m t", t=PACK),
+            w4_plane[:].rearrange("p a (b m t) -> p (a b) m t", b=R_PASSES, t=PACK),
+        )
+
+        scores = [
+            [psum.tile([P, 2, HALF], F32, name=f"scores{half}{pair}") for pair in range(2)] for half in range(2)
+        ]
+        w2_mx = {}
+        x_rows = {}
+
+        def first_stage(b, t):
+            cols = slice(t * P, (t + 1) * P)
+            angle = psum.tile([P, S], F32, name="angle", bufs=2)
+            for a in range(K_PASSES):
+                codes, scales = w1_mx[a, b]
+                nc.tensor.matmul_mx(
+                    angle[:], codes[:, cols].bitcast(FP8X4), scales[:, cols],
+                    v_words[a][:].bitcast(FP8X4), v_scales[a][:], start=(a == 0), stop=(a == K_PASSES - 1),
+                )
+            b_sum = psum.tile([P, S], F32, name="b_sum", bufs=2)
+            for a in range(K_PASSES):
+                g = a * R_PASSES + b
+                nc.tensor.matmul_mx(
+                    b_sum[:], w4_codes[:, g, 2 * t * P : 2 * (t + 1) * P].bitcast(FP4X4), w4_sc[:, g, cols],
+                    v_words[a][:].bitcast(FP8X4), v_scales[a][:], start=(a == 0), stop=(a == K_PASSES - 1),
+                )
+            turns = ring.tile([P, S], F32, name="turns", bufs=3)
+            nc.scalar.activation(turns[:], angle[:], ACT.Abs, scale=1.0 / (2.0 * math.pi))
+            factor = ring.tile([P, S], F32, name="factor", bufs=4)
+            g_col = minus_gain[:, b, t : t + 1]
+            nc.scalar.activation(factor[:], b_sum[:], ACT.Identity, bias=g_col, scale=g_col)
+            whole = ring.tile([P, S], U32, name="whole")
+            nc.scalar.copy(whole[:], turns[:])
+            rest = ring.tile([P, S], F32, name="rest", bufs=3)
+            nc.vector.tensor_tensor(rest[:], turns[:], whole[:].bitcast(I32), ALU.subtract)
+            return rest, factor, turns
+
+        def make_h(rest, factor, h):
+            sine = ring.tile([P, S], F32, name="sine")
+            nc.scalar.activation(sine[:], rest[:], ACT.Sin, scale=math.pi)
+            versine = ring.tile([P, S], F32, name="versine")
+            nc.scalar.activation(versine[:], sine[:], ACT.Square, scale=math.sqrt(2.0))
+            nc.vector.scalar_tensor_tensor(h[:], versine[:], 1.0, factor[:], ALU.subtract, ALU.mult)
+            return h
+
+        def second_stage(b):
+            codes_w, scales_w = w2_mx[b]
+            for half in range(2):
+                woven = ring.tile([P, HALF, PACK], BF16, name="woven", align_bytes=64)
+                engine_copy = nc.vector.tensor_copy if (b, half) == (1, 1) else nc.scalar.copy
+                engine_copy(
+                    woven[:].rearrange("p (c i) t -> p c t i", i=4),
+                    x_rows[b][:, :, half * HALF : (half + 1) * HALF].rearrange("p t (c i) -> p c t i", i=4),
+                )
+                codes = ring.tile([P, HALF], U32, name="x_codes", align_bytes=64)
+                scales = ring.tile([P, HALF], U8, name="x_scales", align_bytes=64)
+                nc.vector.quantize_mx(codes[:].bitcast(FP8X4), scales[:], woven[:].rearrange("p m t -> p (m t)"))
+                for t in range(PACK):
+                    cols = slice(t * P, (t + 1) * P)
+                    nc.tensor.matmul_mx(
+                        scores[half][t // 2][:, t % 2, :], codes_w[:, cols].bitcast(FP8X4), scales_w[:, cols],
+                        codes[:].bitcast(FP8X4), scales[:],
+                        start=(b == 0 and t % 2 == 0), stop=(b == R_PASSES - 1 and t % 2 == 1),
+                    )
+
+        before = {}
+        for b, t in slices:
+            before[b, t] = keep.tile([P, PICKS], F32, name=f"before{b}{t}")
+            nc.vector.tensor_copy(before[b, t][:], pages[b, t][:].indirect(before_list[:]))
+
+        staged = {0: first_stage(*slices[0]), 1: first_stage(*slices[1])}
+        h_next = make_h(*staged[0][:2], staged[1][2])
+        for i, (b, t) in enumerate(slices):
+            h = h_next
+            if i == 1:
+                for a in range(K_PASSES):
+                    w1_mx[a, 1] = quantize_weight(w1_raw[a, 1], f"w1_{a}1")
+            if i == 3 or i == 4:
+                w2_mx[i - 3] = quantize_weight(w2_raw[i - 3], f"w2_{i - 3}")
+            if t == 0:
+                x_rows[b] = keep.tile([P, PACK, PICKS], BF16, name=f"x_rows{b}")
+            nc.vector.tensor_tensor(pages[b, t][:].indirect(put_list[:]), h[:], wgs_sb[:, t, :], ALU.mult)
+            if i + 2 < len(slices):
+                staged[i + 2] = first_stage(*slices[i + 2])
+            after = ring.tile([P, PICKS], F32, name="after")
+            nc.vector.tensor_copy(after[:], pages[b, t][:].indirect(after_list[:]))
+            if i + 2 < len(slices):
+                h_next = make_h(*staged[i + 1][:2], staged[i + 2][2])
+            elif i + 1 < len(slices):
+                h_next = make_h(*staged[i + 1][:2], ring.tile([P, S], F32, name="turns", bufs=3))
+            nc.vector.tensor_tensor(x_rows[b][:, t, :], after[:], before[b, t][:], ALU.min)
+            if t == PACK - 1:
+                second_stage(b)
+
+        out_rows = out.rearrange("(p t) m -> p t m", t=PACK)
+        for half in range(2):
+            for pair in range(2):
+                result = keep.tile([P, 2, HALF], F32, name=f"result{half}{pair}")
+                for u in range(2):
+                    t = 2 * pair + u
+                    if pair == 0:
+                        nc.scalar.activation(
+                            result[:, u, :], scores[half][pair][:, u, :], ACT.Identity, bias=bias_sb[:, t : t + 1]
+                        )
+                    else:
+                        nc.vector.tensor_scalar_add(result[:, u, :], scores[half][pair][:, u, :], bias_sb[:, t : t + 1])
+                nc.sync.dma_start(out_rows[:, 2 * pair : 2 * pair + 2, half * HALF : (half + 1) * HALF], result[:])

@@ -2,6 +2,7 @@ import math
 from contextlib import ExitStack
 
 import concourse.mybir as mybir
+from concourse.masks import make_identity
 
 K, T, S, H, T2, PICKS, N = 1024, 2048, 512, 1024, 1024, 512, 512
 FLOPS = 2 * (2 * K * H * S + H * N * PICKS)
@@ -45,21 +46,21 @@ def tile_list_lining_tapping_scores_kernel(
             return raw
 
         def quantize_weight(raw, name):
-            dealt = ring.tile([P, PACK, P, PACK], BF16, name="dealt", align_bytes=64)
+            dealt = keep.tile([P, PACK, P, PACK], BF16, name=name + "_dealt", align_bytes=64)
             nc.scalar.copy(
                 dealt[:].rearrange("p t m j -> p m j t"), raw[:].rearrange("p j (m t) -> p m j t", t=PACK)
             )
             codes = keep.tile([P, PASS], U32, name=name + "_codes", align_bytes=64)
             scales = keep.tile([P, PASS], U8, name=name + "_scales", align_bytes=64)
             nc.vector.quantize_mx(codes[:].bitcast(FP8X4), scales[:], dealt[:].rearrange("p t m j -> p (t m j)"))
-            return codes, scales
+            return codes, scales, dealt
 
         def load_scale_rows(source, width, name):
             plane = keep.tile([P, K_PASSES, width], U8, name=name, align_bytes=64)
             nc.vector.memset(plane[:].bitcast(I32), 0)
             rows = source.rearrange("a q c -> q a c").bitcast(I32)
             for quad in range(4):
-                nc.scalar.dma_start(plane[32 * quad : 32 * quad + 4].bitcast(I32), rows[4 * quad : 4 * quad + 4])
+                nc.sync.dma_start(plane[32 * quad : 32 * quad + 4].bitcast(I32), rows[4 * quad : 4 * quad + 4])
             return plane
 
         def load_table(a):
@@ -74,52 +75,62 @@ def tile_list_lining_tapping_scores_kernel(
 
         slices = [(b, t) for b in range(R_PASSES) for t in range(PACK)]
 
-        table_plane = load_scale_rows(tab_scales, T, "table_plane")
-        w4_plane = load_scale_rows(w4_scales, H, "w4_plane")
-        gain_sb = keep.tile([P, R_PASSES, PACK], F32, name="gain_sb")
-        nc.scalar.dma_start(gain_sb[:], gain.rearrange("(b p t) -> p b t", p=P, t=PACK))
-        bias_sb = keep.tile([P, PACK], F32, name="bias_sb")
-        nc.scalar.dma_start(bias_sb[:], bias.rearrange("(p t) -> p t", t=PACK))
-
-        picked = load_list(offs, "picked")
-        w1_raw = {}
-        table = {}
-        table[0] = load_table(0)
-        w1_raw[0, 0] = load_weight(w1[0:PASS, 0:PASS], "w1_raw00")
-        w4_raw = keep.tile([P, K_PASSES, 2 * H], U8, name="w4_raw")
-        nc.sync.dma_start(w4_raw[:].bitcast(I32), w4_words.rearrange("a p c -> p a c").bitcast(I32))
-        w1_raw[1, 0] = load_weight(w1[PASS : 2 * PASS, 0:PASS], "w1_raw10")
-        table[1] = load_table(1)
         before_list = load_list(offs4, "before_list")
         pages = {}
         pages[0, 0] = load_page(0, 0)
+        picked = load_list(offs, "picked")
+        table = {}
+        table[0] = load_table(0)
         put_list = load_list(offs2, "put_list")
         after_list = load_list(offs3, "after_list")
-        pages[0, 1] = load_page(0, 1)
+        gain_sb = keep.tile([P, R_PASSES, PACK], F32, name="gain_sb")
+        nc.sync.dma_start(gain_sb[:], gain.rearrange("(b p t) -> p b t", p=P, t=PACK))
+        bias_sb = keep.tile([P, PACK], F32, name="bias_sb")
+        nc.sync.dma_start(bias_sb[:], bias.rearrange("(p t) -> p t", t=PACK))
+        table_plane = keep.tile([P, T], U8, name="table_plane")
+        nc.vector.memset(table_plane[:].bitcast(I32), 0)
+        for quad in range(4):
+            nc.sync.dma_start(
+                table_plane[32 * quad : 32 * quad + 8].bitcast(I32),
+                tab_scales[:, 4 * quad : 4 * quad + 4, :].bitcast(I32),
+            )
+        w1_raw = {}
+        w1_raw[0, 0] = load_weight(w1[0:PASS, 0:PASS], "w1_raw00")
+        w4_raw = keep.tile([P, K_PASSES, 2 * H], U8, name="w4_raw")
+        nc.sync.dma_start(w4_raw[:].bitcast(I32), w4_words.rearrange("a p c -> p a c").bitcast(I32))
+        w4_plane = load_scale_rows(w4_scales, H, "w4_plane")
+        w1_raw[1, 0] = load_weight(w1[PASS : 2 * PASS, 0:PASS], "w1_raw10")
+        table[1] = load_table(1)
+        for b, t in slices[1:-2]:
+            pages[b, t] = load_page(b, t)
         wgs_sb = keep.tile([P, PACK, S], F32, name="wgs_sb")
         for quad in range(4):
             nc.sync.dma_start(wgs_sb[32 * quad : 32 * quad + 32], wgs.rearrange("(u t) j -> u t j", t=PACK))
-        pages[0, 2] = load_page(0, 2)
-        pages[0, 3] = load_page(0, 3)
         for a in range(K_PASSES):
             w1_raw[a, 1] = load_weight(w1[a * PASS : (a + 1) * PASS, PASS : 2 * PASS], f"w1_raw{a}1")
-        for t in range(PACK):
-            pages[1, t] = load_page(1, t)
+        for b, t in slices[-2:]:
+            pages[b, t] = load_page(b, t)
         w2_raw = [load_weight(w2[b * PASS : (b + 1) * PASS, :], f"w2_raw{b}") for b in range(R_PASSES)]
 
         minus_gain = keep.tile([P, R_PASSES, PACK], F32, name="minus_gain")
         nc.scalar.mul(minus_gain[:], gain_sb[:], -1.0)
 
         w1_mx = {}
-        v_words, v_scales = [], []
+        v_plane = keep.tile([P, S], U8, name="v_plane", align_bytes=64)
+        nc.vector.tensor_copy(v_plane[:], table_plane[:].indirect(picked[:]))
+        v_plane_1 = keep.tile([P, S], U8, name="v_plane_1", align_bytes=64)
+        nc.vector.memset(v_plane_1[:].bitcast(I32), 0)
+        for quad in range(4):
+            nc.gpsimd.dma_start(
+                v_plane_1[32 * quad : 32 * quad + 4].bitcast(I32), v_plane[32 * quad + 4 : 32 * quad + 8].bitcast(I32)
+            )
+        v_scales = [v_plane, v_plane_1]
+        v_words = []
         for a in range(K_PASSES):
             w1_mx[a, 0] = quantize_weight(w1_raw[a, 0], f"w1_{a}0")
             words = keep.tile([P, S], U32, name=f"v_words{a}", align_bytes=64)
             nc.vector.tensor_copy(words[:], table[a][:].indirect(picked[:]))
-            scales = keep.tile([P, S], U8, name=f"v_scales{a}", align_bytes=64)
-            nc.vector.tensor_copy(scales[:], table_plane[:, a, :].indirect(picked[:]))
             v_words.append(words)
-            v_scales.append(scales)
 
         w4_codes = keep.tile([P, K_PASSES * R_PASSES, 2 * PASS], U8, name="w4_codes", align_bytes=64)
         nc.vector.tensor_copy(
@@ -138,53 +149,78 @@ def tile_list_lining_tapping_scores_kernel(
         w2_mx = {}
         x_rows = {}
 
+        identity = keep.tile([P, P], F32, name="identity")
+        make_identity(nc, identity[:])
+
         def first_stage(b, t):
+            i = PACK * b + t
             cols = slice(t * P, (t + 1) * P)
-            angle = psum.tile([P, S], F32, name="angle", bufs=2)
-            for a in range(K_PASSES):
-                codes, scales = w1_mx[a, b]
-                nc.tensor.matmul_mx(
-                    angle[:], codes[:, cols].bitcast(FP8X4), scales[:, cols],
-                    v_words[a][:].bitcast(FP8X4), v_scales[a][:], start=(a == 0), stop=(a == K_PASSES - 1),
-                )
-            b_sum = psum.tile([P, S], F32, name="b_sum", bufs=2)
+            angle = psum.tile([P, PACK, P], F32, name="angle")
+            if i == 0:
+                for a in range(K_PASSES):
+                    codes, scales = w1_mx[a, b][:2]
+                    nc.tensor.matmul_mx(
+                        angle[:].rearrange("p a b -> p (a b)"), codes[:, cols].bitcast(FP8X4), scales[:, cols],
+                        v_words[a][:].bitcast(FP8X4), v_scales[a][:], start=(a == 0), stop=(a == K_PASSES - 1),
+                    )
+            else:
+                for jb in range(S // P):
+                    entries = slice(jb * P, (jb + 1) * P)
+                    for a in range(K_PASSES):
+                        codes, scales = w1_mx[a, b][:2]
+                        nc.tensor.matmul_mx(
+                            angle[:, jb, :], v_words[a][:, entries].bitcast(FP8X4), v_scales[a][:, entries],
+                            codes[:, cols].bitcast(FP8X4), scales[:, cols], start=(a == 0), stop=(a == K_PASSES - 1),
+                        )
+            b_sum = psum.tile([P, S], F32, name="b_sum")
             for a in range(K_PASSES):
                 g = a * R_PASSES + b
                 nc.tensor.matmul_mx(
                     b_sum[:], w4_codes[:, g, 2 * t * P : 2 * (t + 1) * P].bitcast(FP4X4), w4_sc[:, g, cols],
                     v_words[a][:].bitcast(FP8X4), v_scales[a][:], start=(a == 0), stop=(a == K_PASSES - 1),
                 )
-            turns = ring.tile([P, S], F32, name="turns", bufs=3)
+            turns = keep.tile([P, PACK, P], F32, name=f"turns{i % 2}" if i else "first_turns", align_bytes=64)
             nc.scalar.activation(turns[:], angle[:], ACT.Abs, scale=1.0 / (2.0 * math.pi))
-            factor = ring.tile([P, S], F32, name="factor", bufs=4)
+            whole = keep.tile([P, PACK, P], U32, name=f"whole{i % 2}" if i else "first_whole")
+            nc.scalar.copy(whole[:], turns[:])
+            factor = keep.tile([P, S], F32, name=f"factor{i % 3}")
             g_col = minus_gain[:, b, t : t + 1]
             nc.scalar.activation(factor[:], b_sum[:], ACT.Identity, bias=g_col, scale=g_col)
-            whole = ring.tile([P, S], U32, name="whole")
-            nc.scalar.copy(whole[:], turns[:])
-            rest = ring.tile([P, S], F32, name="rest", bufs=3)
-            nc.vector.tensor_tensor(rest[:], turns[:], whole[:].bitcast(I32), ALU.subtract)
-            return rest, factor, turns
+            minus_whole = keep.tile([P, PACK, P], F32, name=f"minus_whole{i % 2}")
+            if i == 0:
+                nc.vector.tensor_tensor(minus_whole[:], turns[:], whole[:].bitcast(I32), ALU.subtract)
+            else:
+                nc.scalar.activation(minus_whole[:], whole[:], ACT.Copy, scale=-1.0)
+            return factor, turns, whole, minus_whole
 
-        def make_h(rest, factor, h):
-            sine = ring.tile([P, S], F32, name="sine")
-            nc.scalar.activation(sine[:], rest[:], ACT.Sin, scale=math.pi)
-            versine = ring.tile([P, S], F32, name="versine")
-            nc.scalar.activation(versine[:], sine[:], ACT.Square, scale=math.sqrt(2.0))
-            nc.vector.scalar_tensor_tensor(h[:], versine[:], 1.0, factor[:], ALU.subtract, ALU.mult)
-            return h
+        def cosine_stage(i, turns, minus_whole, sine):
+            if i == 0:
+                rest = minus_whole[:].rearrange("p a b -> p (a b)")
+            else:
+                rest = psum.tile([P, S], F32, name=f"rest{i % 2}")[:]
+            for jb in range(S // P if i > 0 else 0):
+                entries = slice(jb * P, (jb + 1) * P)
+                nc.tensor.matmul(rest[:, entries], turns[:, jb, :], identity[:], start=True, stop=False, is_transpose=True)
+                nc.tensor.matmul(
+                    rest[:, entries], minus_whole[:, jb, :], identity[:], start=False, stop=True, is_transpose=True
+                )
+            nc.scalar.activation(sine, rest, ACT.Sin, scale=math.pi)
+            versine = keep.tile([P, S], F32, name=f"versine{i % 3}")
+            nc.scalar.activation(versine[:], sine, ACT.Square, scale=math.sqrt(2.0))
+            return versine
 
-        def second_stage(b):
-            codes_w, scales_w = w2_mx[b]
+        def second_stage(b, rooms):
+            codes_w, scales_w = w2_mx[b][:2]
             for half in range(2):
-                woven = ring.tile([P, HALF, PACK], BF16, name="woven", align_bytes=64)
+                woven = rooms[half].bitcast(BF16).rearrange("p (m t) -> p m t", t=PACK)
                 engine_copy = nc.vector.tensor_copy if (b, half) == (1, 1) else nc.scalar.copy
                 engine_copy(
-                    woven[:].rearrange("p (c i) t -> p c t i", i=4),
+                    woven.rearrange("p (c i) t -> p c t i", i=4),
                     x_rows[b][:, :, half * HALF : (half + 1) * HALF].rearrange("p t (c i) -> p c t i", i=4),
                 )
-                codes = ring.tile([P, HALF], U32, name="x_codes", align_bytes=64)
-                scales = ring.tile([P, HALF], U8, name="x_scales", align_bytes=64)
-                nc.vector.quantize_mx(codes[:].bitcast(FP8X4), scales[:], woven[:].rearrange("p m t -> p (m t)"))
+                codes = keep.tile([P, HALF], U32, name=f"x_codes{b}{half}", align_bytes=64)
+                scales = keep.tile([P, HALF], U8, name=f"x_scales{b}{half}", align_bytes=64)
+                nc.vector.quantize_mx(codes[:].bitcast(FP8X4), scales[:], rooms[half].bitcast(BF16))
                 for t in range(PACK):
                     cols = slice(t * P, (t + 1) * P)
                     nc.tensor.matmul_mx(
@@ -193,34 +229,55 @@ def tile_list_lining_tapping_scores_kernel(
                         start=(b == 0 and t % 2 == 0), stop=(b == R_PASSES - 1 and t % 2 == 1),
                     )
 
+        staged = first_stage(*slices[0])
         before = {}
-        for b, t in slices:
-            before[b, t] = keep.tile([P, PICKS], F32, name=f"before{b}{t}")
-            nc.vector.tensor_copy(before[b, t][:], pages[b, t][:].indirect(before_list[:]))
-
-        staged = {0: first_stage(*slices[0]), 1: first_stage(*slices[1])}
-        h_next = make_h(*staged[0][:2], staged[1][2])
         for i, (b, t) in enumerate(slices):
-            h = h_next
-            if i == 1:
+            name = {2: "first_turns", 3: "first_whole"}.get(i, f"before{i}")
+            before[b, t] = keep.tile([P, PICKS], F32, name=name, align_bytes=64 if i == 2 else None)
+            nc.vector.tensor_copy(before[b, t][:], pages[b, t][:].indirect(before_list[:]))
+        for b in range(R_PASSES):
+            x_rows[b] = keep.tile([P, PACK, PICKS], BF16, name=f"x_rows{b}")
+
+        for i, (b, t) in enumerate(slices):
+            if i == 2:
                 for a in range(K_PASSES):
                     w1_mx[a, 1] = quantize_weight(w1_raw[a, 1], f"w1_{a}1")
             if i == 3 or i == 4:
                 w2_mx[i - 3] = quantize_weight(w2_raw[i - 3], f"w2_{i - 3}")
-            if t == 0:
-                x_rows[b] = keep.tile([P, PACK, PICKS], BF16, name=f"x_rows{b}")
-            nc.vector.tensor_tensor(pages[b, t][:].indirect(put_list[:]), h[:], wgs_sb[:, t, :], ALU.mult)
-            if i + 2 < len(slices):
-                staged[i + 2] = first_stage(*slices[i + 2])
-            after = ring.tile([P, PICKS], F32, name="after")
-            nc.vector.tensor_copy(after[:], pages[b, t][:].indirect(after_list[:]))
-            if i + 2 < len(slices):
-                h_next = make_h(*staged[i + 1][:2], staged[i + 2][2])
-            elif i + 1 < len(slices):
-                h_next = make_h(*staged[i + 1][:2], ring.tile([P, S], F32, name="turns", bufs=3))
-            nc.vector.tensor_tensor(x_rows[b][:, t, :], after[:], before[b, t][:], ALU.min)
-            if t == PACK - 1:
-                second_stage(b)
+            factor, turns, whole, minus_whole = staged
+            if 0 < i < len(slices) - 1:
+                staged = first_stage(*slices[i + 1])
+            if 1 < i < len(slices) - 1:
+                sine = staged[2][:].rearrange("p a b -> p (a b)").bitcast(F32)
+            else:
+                sine = keep.tile([P, S], F32, name="sine", align_bytes=64)[:]
+            versine = cosine_stage(i, turns, minus_whole, sine)
+            if i == 0:
+                staged = first_stage(*slices[1])
+            spent = [turns[:].rearrange("p a b -> p (a b)"), sine]
+            if i == 2:
+                h = w1_mx[1, 1][2][:].rearrange("p t m j -> p (t m j)").bitcast(F32)[:, 0:S]
+            else:
+                h = keep.tile([P, S], F32, name=f"h{i % 2}")[:]
+            nc.vector.scalar_tensor_tensor(h, versine[:], 1.0, factor[:], ALU.subtract, ALU.mult)
+            if i > 0:
+                last = slices[i - 1]
+                after = versine
+                nc.vector.tensor_copy(after[:], pages[last][:].indirect(after_list[:]))
+            nc.vector.tensor_tensor(pages[b, t][:].indirect(put_list[:]), h, wgs_sb[:, t, :], ALU.mult)
+            if i > 0:
+                nc.vector.tensor_tensor(x_rows[last[0]][:, last[1], :], after[:], before[last][:], ALU.min)
+        second_stage(0, spent)
+        last = slices[-1]
+        after_halves = []
+        for half in range(2):
+            after = ring.tile([P, HALF], F32, name="after_half")
+            nc.vector.tensor_copy(after[:], pages[last][:].indirect(after_list[:, half * 16 : (half + 1) * 16]))
+            after_halves.append(after)
+        for half in range(2):
+            cols = slice(half * HALF, (half + 1) * HALF)
+            nc.vector.tensor_tensor(x_rows[1][:, PACK - 1, cols], after_halves[half][:], before[last][:, cols], ALU.min)
+        second_stage(1, [keep.tile([P, S], F32, name=f"woven{half}", align_bytes=64)[:] for half in range(2)])
 
         out_rows = out.rearrange("(p t) m -> p t m", t=PACK)
         for half in range(2):

import math
from contextlib import ExitStack

import concourse.mybir as mybir
from concourse.masks import make_identity

K, T, S, H, T2, PICKS, N = 1024, 2048, 512, 1024, 1024, 512, 512
FLOPS = 2 * (2 * K * H * S + H * N * PICKS)

F32 = mybir.dt.float32
BF16 = mybir.dt.bfloat16
I32 = mybir.dt.int32
U32 = mybir.dt.uint32
U16 = mybir.dt.uint16
U8 = mybir.dt.uint8
FP8X4 = mybir.dt.float8_e4m3fn_x4
FP4X4 = mybir.dt.float4_e2m1fn_x4
ALU = mybir.AluOpType
ACT = mybir.ActivationFunctionType

P = 128
PACK = 4
PASS = P * PACK
K_PASSES = K // PASS
R_PASSES = H // PASS
HALF = PICKS // 2


def tile_list_lining_tapping_scores_kernel(
    tc, tab_words, tab_scales, w1, w4_words, w4_scales, gain, page0, wgs, w2, bias, offs, offs2, offs3, offs4, out
):
    nc = tc.nc
    with ExitStack() as ctx:
        keep = ctx.enter_context(tc.tile_pool(name="keep", bufs=1))
        ring = ctx.enter_context(tc.tile_pool(name="ring", bufs=2))
        psum = ctx.enter_context(tc.psum_pool(name="psum", bufs=1))

        def load_list(source, name):
            tile = keep.tile([P, S // 16], U16, name=name)
            nc.sync.dma_start(tile[:], source)
            return tile

        def load_weight(rows, name):
            raw = ring.tile([P, PACK, PASS], F32, name=name, tag="raw", bufs=4)
            nc.sync.dma_start(raw[:], rows.rearrange("(p j) c -> p j c", j=PACK))
            return raw

        def quantize_weight(raw, name):
            dealt = keep.tile([P, PACK, P, PACK], BF16, name=name + "_dealt", align_bytes=64)
            nc.scalar.copy(
                dealt[:].rearrange("p t m j -> p m j t"), raw[:].rearrange("p j (m t) -> p m j t", t=PACK)
            )
            codes = keep.tile([P, PASS], U32, name=name + "_codes", align_bytes=64)
            scales = keep.tile([P, PASS], U8, name=name + "_scales", align_bytes=64)
            nc.vector.quantize_mx(codes[:].bitcast(FP8X4), scales[:], dealt[:].rearrange("p t m j -> p (t m j)"))
            return codes, scales, dealt

        def load_scale_rows(source, width, name):
            plane = keep.tile([P, K_PASSES, width], U8, name=name, align_bytes=64)
            nc.vector.memset(plane[:].bitcast(I32), 0)
            rows = source.rearrange("a q c -> q a c").bitcast(I32)
            for quad in range(4):
                nc.sync.dma_start(plane[32 * quad : 32 * quad + 4].bitcast(I32), rows[4 * quad : 4 * quad + 4])
            return plane

        def load_table(a):
            words = keep.tile([P, T], U32, name=f"table{a}")
            nc.sync.dma_start(words[:].bitcast(I32), tab_words[a].rearrange("p t i -> p (t i)").bitcast(I32))
            return words

        def load_page(b, t):
            page = keep.tile([P, T2], F32, name=f"page{b}{t}")
            nc.sync.dma_start(page[:], page0.rearrange("(b p t) c -> b t p c", p=P, t=PACK)[b, t])
            return page

        slices = [(b, t) for b in range(R_PASSES) for t in range(PACK)]

        before_list = load_list(offs4, "before_list")
        pages = {}
        pages[0, 0] = load_page(0, 0)
        picked = load_list(offs, "picked")
        table = {}
        table[0] = load_table(0)
        put_list = load_list(offs2, "put_list")
        after_list = load_list(offs3, "after_list")
        gain_sb = keep.tile([P, R_PASSES, PACK], F32, name="gain_sb")
        nc.sync.dma_start(gain_sb[:], gain.rearrange("(b p t) -> p b t", p=P, t=PACK))
        bias_sb = keep.tile([P, PACK], F32, name="bias_sb")
        nc.sync.dma_start(bias_sb[:], bias.rearrange("(p t) -> p t", t=PACK))
        table_plane = keep.tile([P, T], U8, name="table_plane")
        nc.vector.memset(table_plane[:].bitcast(I32), 0)
        for quad in range(4):
            nc.sync.dma_start(
                table_plane[32 * quad : 32 * quad + 8].bitcast(I32),
                tab_scales[:, 4 * quad : 4 * quad + 4, :].bitcast(I32),
            )
        w1_raw = {}
        w1_raw[0, 0] = load_weight(w1[0:PASS, 0:PASS], "w1_raw00")
        w4_raw = keep.tile([P, K_PASSES, 2 * H], U8, name="w4_raw")
        nc.sync.dma_start(w4_raw[:].bitcast(I32), w4_words.rearrange("a p c -> p a c").bitcast(I32))
        w4_plane = load_scale_rows(w4_scales, H, "w4_plane")
        w1_raw[1, 0] = load_weight(w1[PASS : 2 * PASS, 0:PASS], "w1_raw10")
        table[1] = load_table(1)
        for b, t in slices[1:-2]:
            pages[b, t] = load_page(b, t)
        wgs_sb = keep.tile([P, PACK, S], F32, name="wgs_sb")
        for quad in range(4):
            nc.sync.dma_start(wgs_sb[32 * quad : 32 * quad + 32], wgs.rearrange("(u t) j -> u t j", t=PACK))
        for a in range(K_PASSES):
            w1_raw[a, 1] = load_weight(w1[a * PASS : (a + 1) * PASS, PASS : 2 * PASS], f"w1_raw{a}1")
        for b, t in slices[-2:]:
            pages[b, t] = load_page(b, t)
        w2_raw = [load_weight(w2[b * PASS : (b + 1) * PASS, :], f"w2_raw{b}") for b in range(R_PASSES)]

        minus_gain = keep.tile([P, R_PASSES, PACK], F32, name="minus_gain")
        nc.scalar.mul(minus_gain[:], gain_sb[:], -1.0)

        w1_mx = {}
        v_plane = keep.tile([P, S], U8, name="v_plane", align_bytes=64)
        nc.vector.tensor_copy(v_plane[:], table_plane[:].indirect(picked[:]))
        v_plane_1 = keep.tile([P, S], U8, name="v_plane_1", align_bytes=64)
        nc.vector.memset(v_plane_1[:].bitcast(I32), 0)
        for quad in range(4):
            nc.gpsimd.dma_start(
                v_plane_1[32 * quad : 32 * quad + 4].bitcast(I32), v_plane[32 * quad + 4 : 32 * quad + 8].bitcast(I32)
            )
        v_scales = [v_plane, v_plane_1]
        v_words = []
        for a in range(K_PASSES):
            w1_mx[a, 0] = quantize_weight(w1_raw[a, 0], f"w1_{a}0")
            words = keep.tile([P, S], U32, name=f"v_words{a}", align_bytes=64)
            nc.vector.tensor_copy(words[:], table[a][:].indirect(picked[:]))
            v_words.append(words)

        w4_codes = keep.tile([P, K_PASSES * R_PASSES, 2 * PASS], U8, name="w4_codes", align_bytes=64)
        nc.vector.tensor_copy(
            w4_codes[:].bitcast(U16).rearrange("p g (t m) -> p g m t", t=PACK),
            w4_raw[:].bitcast(U16).rearrange("p a (b m t) -> p (a b) m t", b=R_PASSES, t=PACK),
        )
        w4_sc = keep.tile([P, K_PASSES * R_PASSES, PASS], U8, name="w4_sc", align_bytes=64)
        nc.vector.tensor_copy(
            w4_sc[:].rearrange("p g (t m) -> p g m t", t=PACK),
            w4_plane[:].rearrange("p a (b m t) -> p (a b) m t", b=R_PASSES, t=PACK),
        )

        scores = [
            [psum.tile([P, 2, HALF], F32, name=f"scores{half}{pair}") for pair in range(2)] for half in range(2)
        ]
        w2_mx = {}
        x_rows = {}

        identity = keep.tile([P, P], F32, name="identity")
        make_identity(nc, identity[:])

        def first_stage(b, t):
            i = PACK * b + t
            cols = slice(t * P, (t + 1) * P)
            angle = psum.tile([P, PACK, P], F32, name="angle")
            if i == 0:
                for a in range(K_PASSES):
                    codes, scales = w1_mx[a, b][:2]
                    nc.tensor.matmul_mx(
                        angle[:].rearrange("p a b -> p (a b)"), codes[:, cols].bitcast(FP8X4), scales[:, cols],
                        v_words[a][:].bitcast(FP8X4), v_scales[a][:], start=(a == 0), stop=(a == K_PASSES - 1),
                    )
            else:
                for jb in range(S // P):
                    entries = slice(jb * P, (jb + 1) * P)
                    for a in range(K_PASSES):
                        codes, scales = w1_mx[a, b][:2]
                        nc.tensor.matmul_mx(
                            angle[:, jb, :], v_words[a][:, entries].bitcast(FP8X4), v_scales[a][:, entries],
                            codes[:, cols].bitcast(FP8X4), scales[:, cols], start=(a == 0), stop=(a == K_PASSES - 1),
                        )
            b_sum = psum.tile([P, S], F32, name="b_sum")
            for a in range(K_PASSES):
                g = a * R_PASSES + b
                nc.tensor.matmul_mx(
                    b_sum[:], w4_codes[:, g, 2 * t * P : 2 * (t + 1) * P].bitcast(FP4X4), w4_sc[:, g, cols],
                    v_words[a][:].bitcast(FP8X4), v_scales[a][:], start=(a == 0), stop=(a == K_PASSES - 1),
                )
            turns = keep.tile([P, PACK, P], F32, name=f"turns{i % 2}" if i else "first_turns", align_bytes=64)
            nc.scalar.activation(turns[:], angle[:], ACT.Abs, scale=1.0 / (2.0 * math.pi))
            whole = keep.tile([P, PACK, P], U32, name=f"whole{i % 2}" if i else "first_whole")
            nc.scalar.copy(whole[:], turns[:])
            factor = keep.tile([P, S], F32, name=f"factor{i % 3}")
            g_col = minus_gain[:, b, t : t + 1]
            nc.scalar.activation(factor[:], b_sum[:], ACT.Identity, bias=g_col, scale=g_col)
            minus_whole = keep.tile([P, PACK, P], F32, name=f"minus_whole{i % 2}")
            if i == 0:
                nc.vector.tensor_tensor(minus_whole[:], turns[:], whole[:].bitcast(I32), ALU.subtract)
            else:
                nc.scalar.activation(minus_whole[:], whole[:], ACT.Copy, scale=-1.0)
            return factor, turns, whole, minus_whole

        def cosine_stage(i, turns, minus_whole, sine):
            if i == 0:
                rest = minus_whole[:].rearrange("p a b -> p (a b)")
            else:
                rest = psum.tile([P, S], F32, name=f"rest{i % 2}")[:]
            for jb in range(S // P if i > 0 else 0):
                entries = slice(jb * P, (jb + 1) * P)
                nc.tensor.matmul(rest[:, entries], turns[:, jb, :], identity[:], start=True, stop=False, is_transpose=True)
                nc.tensor.matmul(
                    rest[:, entries], minus_whole[:, jb, :], identity[:], start=False, stop=True, is_transpose=True
                )
            nc.scalar.activation(sine, rest, ACT.Sin, scale=math.pi)
            versine = keep.tile([P, S], F32, name=f"versine{i % 3}")
            nc.scalar.activation(versine[:], sine, ACT.Square, scale=math.sqrt(2.0))
            return versine

        def second_stage(b, rooms):
            codes_w, scales_w = w2_mx[b][:2]
            for half in range(2):
                woven = rooms[half].bitcast(BF16).rearrange("p (m t) -> p m t", t=PACK)
                engine_copy = nc.vector.tensor_copy if (b, half) == (1, 1) else nc.scalar.copy
                engine_copy(
                    woven.rearrange("p (c i) t -> p c t i", i=4),
                    x_rows[b][:, :, half * HALF : (half + 1) * HALF].rearrange("p t (c i) -> p c t i", i=4),
                )
                codes = keep.tile([P, HALF], U32, name=f"x_codes{b}{half}", align_bytes=64)
                scales = keep.tile([P, HALF], U8, name=f"x_scales{b}{half}", align_bytes=64)
                nc.vector.quantize_mx(codes[:].bitcast(FP8X4), scales[:], rooms[half].bitcast(BF16))
                for t in range(PACK):
                    cols = slice(t * P, (t + 1) * P)
                    nc.tensor.matmul_mx(
                        scores[half][t // 2][:, t % 2, :], codes_w[:, cols].bitcast(FP8X4), scales_w[:, cols],
                        codes[:].bitcast(FP8X4), scales[:],
                        start=(b == 0 and t % 2 == 0), stop=(b == R_PASSES - 1 and t % 2 == 1),
                    )

        staged = first_stage(*slices[0])
        before = {}
        for i, (b, t) in enumerate(slices):
            name = {2: "first_turns", 3: "first_whole"}.get(i, f"before{i}")
            before[b, t] = keep.tile([P, PICKS], F32, name=name, align_bytes=64 if i == 2 else None)
            nc.vector.tensor_copy(before[b, t][:], pages[b, t][:].indirect(before_list[:]))
        for b in range(R_PASSES):
            x_rows[b] = keep.tile([P, PACK, PICKS], BF16, name=f"x_rows{b}")

        for i, (b, t) in enumerate(slices):
            if i == 2:
                for a in range(K_PASSES):
                    w1_mx[a, 1] = quantize_weight(w1_raw[a, 1], f"w1_{a}1")
            if i == 3 or i == 4:
                w2_mx[i - 3] = quantize_weight(w2_raw[i - 3], f"w2_{i - 3}")
            factor, turns, whole, minus_whole = staged
            if 0 < i < len(slices) - 1:
                staged = first_stage(*slices[i + 1])
            if 1 < i < len(slices) - 1:
                sine = staged[2][:].rearrange("p a b -> p (a b)").bitcast(F32)
            else:
                sine = keep.tile([P, S], F32, name="sine", align_bytes=64)[:]
            versine = cosine_stage(i, turns, minus_whole, sine)
            if i == 0:
                staged = first_stage(*slices[1])
            spent = [turns[:].rearrange("p a b -> p (a b)"), sine]
            if i == 2:
                h = w1_mx[1, 1][2][:].rearrange("p t m j -> p (t m j)").bitcast(F32)[:, 0:S]
            else:
                h = keep.tile([P, S], F32, name=f"h{i % 2}")[:]
            nc.vector.scalar_tensor_tensor(h, versine[:], 1.0, factor[:], ALU.subtract, ALU.mult)
            if i > 0:
                last = slices[i - 1]
                after = versine
                nc.vector.tensor_copy(after[:], pages[last][:].indirect(after_list[:]))
            nc.vector.tensor_tensor(pages[b, t][:].indirect(put_list[:]), h, wgs_sb[:, t, :], ALU.mult)
            if i > 0:
                nc.vector.tensor_tensor(x_rows[last[0]][:, last[1], :], after[:], before[last][:], ALU.min)
        second_stage(0, spent)
        last = slices[-1]
        after_halves = []
        for half in range(2):
            after = ring.tile([P, HALF], F32, name="after_half")
            nc.vector.tensor_copy(after[:], pages[last][:].indirect(after_list[:, half * 16 : (half + 1) * 16]))
            after_halves.append(after)
        for half in range(2):
            cols = slice(half * HALF, (half + 1) * HALF)
            nc.vector.tensor_tensor(x_rows[1][:, PACK - 1, cols], after_halves[half][:], before[last][:, cols], ALU.min)
        second_stage(1, [keep.tile([P, S], F32, name=f"woven{half}", align_bytes=64)[:] for half in range(2)])

        out_rows = out.rearrange("(p t) m -> p t m", t=PACK)
        for half in range(2):
            for pair in range(2):
                result = keep.tile([P, 2, HALF], F32, name=f"result{half}{pair}")
                for u in range(2):
                    t = 2 * pair + u
                    if pair == 0:
                        nc.scalar.activation(
                            result[:, u, :], scores[half][pair][:, u, :], ACT.Identity, bias=bias_sb[:, t : t + 1]
                        )
                    else:
                        nc.vector.tensor_scalar_add(result[:, u, :], scores[half][pair][:, u, :], bias_sb[:, t : t + 1])
                nc.sync.dma_start(out_rows[:, 2 * pair : 2 * pair + 2, half * HALF : (half + 1) * HALF], result[:])
